import numpy as np
import ml_dtypes


def mxq(x, axis, fmt="e4m3"):
    dtype, down = {"e4m3": (ml_dtypes.float8_e4m3fn, 7), "e5m2": (ml_dtypes.float8_e5m2, 14)}[fmt]
    v = np.moveaxis(np.asarray(x, np.float32).astype(ml_dtypes.bfloat16).astype(np.float64), axis, -1)
    blocks = v.reshape(v.shape[:-1] + (-1, 32))
    amax = np.abs(blocks).max(-1, keepdims=True)
    byte = np.maximum(np.where(amax > 0, np.frexp(amax)[1] - 1 + 127, 0) - down, 1)
    scale = np.exp2(byte - 127.0)
    codes = (blocks / scale).astype(np.float32).astype(dtype).astype(np.float64)
    return np.moveaxis((codes * scale).reshape(v.shape), -1, axis)


WIDE = False


def mx_kscale(k):
    if not WIDE:
        return np.ones(k)
    levels = np.array([10, -10, 5, -5, 0])
    if k % 512:
        return np.exp2(np.random.permutation(np.resize(levels, k // 32))).repeat(32)
    a = np.empty((k // 512, 16))
    for p in range(k // 512):
        a[p, :8] = np.random.permutation(np.resize(levels, 8))
        for g in range(8):
            far = levels[np.abs(levels - a[p, g]) >= 10]
            a[p, g + 8] = far[np.random.randint(len(far))]
    return np.exp2(a.ravel()).repeat(32)


BF16 = ml_dtypes.bfloat16


def bf(x):
    return np.asarray(x, np.float32).astype(BF16)


def f64(x):
    return np.asarray(x).astype(np.float64)


B, D = 512, 1536


def sigmoid(v):
    return 1.0 / (1.0 + np.exp(-v))


def draw0():
    s = mx_kscale(D)
    t = mx_kscale(D)
    return {"x": bf(np.random.standard_normal((B, D)) * s[None, :]),
            "wg": bf(np.random.standard_normal((D, D)) / np.sqrt(D) / s[:, None]),
            "wc1": bf(np.random.standard_normal((D, D)) / np.sqrt(D) / s[:, None]),
            "gm": bf((1.0 + 0.1 * np.random.standard_normal(D)) * t / s),
            "wc2": bf(np.random.standard_normal((D, D)) / np.sqrt(D) / t[:, None])}


def core(x, wg, wc1, gm, wc2):
    x = f64(x)
    xq = mxq(x, 1, "e4m3")
    xg = x * sigmoid(xq @ mxq(f64(wg), 0, "e4m3"))
    f1 = xq @ mxq(f64(wc1), 0, "e4m3")
    c1 = xg * f1 + x
    u = c1 * f64(gm)[None, :]
    f2 = mxq(u, 1, "e4m3") @ mxq(f64(wc2), 0, "e4m3")
    return xg * f2 + c1


def e4m3fn_bytes(y):
    return np.clip(np.asarray(y, np.float64), -448.0, 448.0).astype(np.float32).astype(ml_dtypes.float8_e4m3fn).view(np.uint8)


def e4m3fn_values(b):
    return np.asarray(b, np.uint8).view(ml_dtypes.float8_e4m3fn).astype(np.float64)


def setup_inputs():
    d = draw0()
    x0 = np.asarray(d['wg']).astype(np.float64)
    s = (np.max(np.abs(x0), axis=(1,), keepdims=True) / 448.0).astype(np.float32)
    out = {}
    for k, v in d.items():
        if k == 'wg':
            out['wg_bytes'] = e4m3fn_bytes(x0 / s.astype(np.float64))
            out['wg_scale'] = s
        else:
            out[k] = v
    return out


def reference(x, wg_bytes, wg_scale, wc1, gm, wc2):
    return core(x, e4m3fn_values(wg_bytes) * wg_scale.astype(np.float64), wc1, gm, wc2)

from contextlib import ExitStack

import concourse.mybir as mybir
from concourse.masks import make_identity

B, D = 512, 1536
P = 128
BLK = 512
NB = D // BLK
MT = B // P
LEAD = 5
IL = "VVHVSVHVHVHVVVVSSSSSVSSSSSS"
WD = "SSSSVSSSS"
XE = "VSSVSV"
XG = "VVSSSVVSSSSS"
GS = 3
HS = 6
FS = 21

F32 = mybir.dt.float32
BF16 = mybir.dt.bfloat16
U32 = mybir.dt.uint32
U8 = mybir.dt.uint8
FP8 = mybir.dt.float8_e4m3fn
FP8X4 = mybir.dt.float8_e4m3fn_x4
ACT = mybir.ActivationFunctionType
ALU = mybir.AluOpType

FLOPS = 3 * 2 * B * D * D + 8 * B * D


def tile_gateddeepcrosstwolayer_kernel(tc, x, wg_bytes, wg_scale, wc1, gm, wc2, out):
    nc = tc.nc
    with ExitStack() as ctx:
        keep = ctx.enter_context(tc.tile_pool(name="keep", bufs=1))
        rawp = ctx.enter_context(tc.tile_pool(name="rawp", bufs=6))
        bytp = ctx.enter_context(tc.tile_pool(name="bytp", bufs=4))
        wgqp = ctx.enter_context(tc.tile_pool(name="wgqp", bufs=2))
        widp = ctx.enter_context(tc.tile_pool(name="widp", bufs=2))
        grpp = ctx.enter_context(tc.tile_pool(name="grpp", bufs=4))
        elem = ctx.enter_context(tc.tile_pool(name="elem", bufs=3))
        acc_pool = ctx.enter_context(tc.psum_pool(name="acc_pool", bufs=6))
        tr_pool = ctx.enter_context(tc.psum_pool(name="tr_pool", bufs=2))

        x_sb = []
        for m in range(MT):
            x_sb.append(keep.tile([P, D], BF16, name=f"x_sb{m}", align_bytes=64))
        ws = keep.tile([P, NB, 4], F32, name="ws")
        gm_raw = keep.tile([P, NB, 4], BF16, name="gm_raw")
        nc.sync.dma_start(out=x_sb[0][:], in_=x[0:P, :])
        nc.sync.dma_start(out=x_sb[1][:], in_=x[P : 2 * P, :])
        nc.sync.dma_start(out=ws[:], in_=wg_scale.rearrange("(g p t) o -> p g (t o)", p=P, t=4))
        nc.sync.dma_start(out=x_sb[2][:], in_=x[2 * P : 3 * P, :])
        nc.sync.dma_start(out=x_sb[3][:], in_=x[3 * P : 4 * P, :])

        units = []
        for j in range(NB):
            for g in range(NB):
                units.append(("wg", j, g))
            for g in range(NB):
                units.append(("wc1", j, g))
        for j in range(NB):
            for g in range(NB):
                units.append(("wc2", j, g))

        raw = {}

        def load(n):
            if n >= len(units):
                return
            w, j, g = units[n]
            src = {"wg": wg_bytes, "wc1": wc1, "wc2": wc2}[w]
            view = src[g * BLK : (g + 1) * BLK, j * BLK : (j + 1) * BLK].rearrange("(p t) n -> p t n", t=4)
            if w == "wg":
                wg_raw = bytp.tile([P, 4, BLK], U8, name="wg_raw")
                raw[n] = wg_raw
            else:
                w_raw = rawp.tile([P, 4, BLK], BF16, name="w_raw")
                raw[n] = w_raw
            nc.sync.dma_start(out=raw[n][:], in_=view)

        for n in range(3):
            load(n)
        nc.sync.dma_start(out=gm_raw[:], in_=gm.rearrange("(g p t) -> p g t", p=P, t=4))
        for n in range(3, LEAD):
            load(n)

        warm = keep.tile([P, 1], F32, name="warm")
        nc.vector.memset(warm[:], 0.0)
        nc.scalar.activation(out=warm[:], in_=warm[:], func=ACT.Sigmoid)
        ident = keep.tile([P, P], F32, name="ident")
        make_identity(nc, ident[:])
        gmf = keep.tile([P, NB, 4], F32, name="gmf")
        nc.vector.tensor_copy(out=gmf[:], in_=gm_raw[:])

        xt = []
        xq = []
        xs = []
        xgm = []
        uq = []
        us = []
        for g in range(NB):
            xt.append(keep.tile([P, B * 4], BF16, name=f"xt{g}", align_bytes=64))
            xq.append(keep.tile([P, B], U32, name=f"xq{g}", align_bytes=64))
            xs.append(keep.tile([P, B], U8, name=f"xs{g}", align_bytes=64))
            xgm.append(keep.tile([P, 4, B], F32, name=f"xgm{g}", align_bytes=64))
            uq.append(keep.tile([P, B], U32, name=f"uq{g}", align_bytes=64))
            us.append(keep.tile([P, B], U8, name=f"us{g}", align_bytes=64))
        s_sb = {}
        for m in range(MT):
            for j in range(NB):
                s_sb[(m, j)] = keep.tile([P, BLK], F32, name=f"s{m}_{j}", align_bytes=64)

        def x_half(mp, g):
            bank = tr_pool.tile([P, 2, 2 * P], F32, name="bank")
            for u in range(2):
                for m in range(2):
                    words = x_sb[2 * mp + m][:].bitcast(F32)
                    nc.tensor.transpose(bank[:, u, m * P : (m + 1) * P], words[:, 256 * g + u : 256 * (g + 1) : 2], ident[:])
            dst = xt[g][:, mp * 1024 : (mp + 1) * 1024].bitcast(F32).rearrange("p (n u) -> p n u", u=2)
            src = bank[:].rearrange("p u n -> p n u")
            if XE[mp * 3 + g] == "S":
                nc.scalar.copy(out=dst, in_=src)
            else:
                nc.vector.tensor_copy(out=dst, in_=src)

        for mp in range(2):
            for g in range(NB):
                x_half(mp, g)
        for g in range(NB):
            nc.vector.quantize_mx(out=xq[g][:].bitcast(FP8X4), scales=xs[g][:], in_=xt[g][:])

        def make_xgm(g, t):
            dst = xgm[g][:, t, :]
            src = xt[g][:].rearrange("p (n t) -> p t n", t=4)[:, t, :]
            if XG[4 * g + t] == "S":
                nc.scalar.activation(out=dst, in_=src, func=ACT.Copy, scale=gmf[:, g, t : t + 1])
            else:
                nc.vector.tensor_scalar(out=dst, in0=src, scalar1=gmf[:, g, t : t + 1], scalar2=None, op0=ALU.mult)

        planes = {}
        grouped = {}
        codes = {}

        def widen(n):
            w, j, g = units[n]
            if w != "wg":
                planes[n] = raw[n]
                return
            wide = widp.tile([P, 4, BLK], BF16, name="wide")
            planes[n] = wide
            for t in range(4):
                if WD[3 * j + g] == "S":
                    nc.scalar.activation(
                        out=wide[:, t, :], in_=raw[n][:, t, :].bitcast(FP8), func=ACT.Copy, scale=ws[:, g, t : t + 1]
                    )
                else:
                    nc.vector.tensor_scalar(
                        out=wide[:, t, :], in0=raw[n][:, t, :].bitcast(FP8), scalar1=ws[:, g, t : t + 1], scalar2=None, op0=ALU.mult
                    )

        def interleave(n):
            w, j, g = units[n]
            grp = grpp.tile([P, 4 * BLK], BF16, name="grp", align_bytes=64)
            grouped[n] = grp
            dst = grp[:].rearrange("p (c i t) -> p c t i", i=4, t=4)
            src = planes[n][:].rearrange("p t (c i) -> p c t i", i=4)
            if IL[n] == "V":
                nc.vector.tensor_copy(out=dst, in_=src)
            elif IL[n] == "S":
                nc.scalar.copy(out=dst, in_=src)
            else:
                h = BLK // 8
                nc.vector.tensor_copy(out=dst[:, :h], in_=src[:, :h])
                nc.scalar.copy(out=dst[:, h:], in_=src[:, h:])

        def quantise(n):
            w, j, g = units[n]
            if w == "wg":
                cq = wgqp.tile([P, BLK], U32, name=f"gq{g}", align_bytes=64)
                cs = wgqp.tile([P, BLK], U8, name=f"gs{g}", align_bytes=64)
            else:
                cq = keep.tile([P, BLK], U32, name=f"{w}q{j}_{g}", align_bytes=64)
                cs = keep.tile([P, BLK], U8, name=f"{w}s{j}_{g}", align_bytes=64)
            codes[(w, j, g)] = (cq, cs)
            nc.vector.quantize_mx(out=cq[:].bitcast(FP8X4), scales=cs[:], in_=grouped[n][:])

        def mm(acc, m, aq, asc, w, j, g, start, stop):
            cols = slice(m * P, (m + 1) * P)
            cq, cs = codes[(w, j, g)]
            nc.tensor.matmul_mx(
                out=acc[:], lhsT=aq[g][:, cols].bitcast(FP8X4), lhsT_scale=asc[g][:, cols],
                rhs=cq[:].bitcast(FP8X4), rhs_scale=cs[:], start=start, stop=stop,
            )

        def gate(m, j):
            acc = acc_pool.tile([P, BLK], F32, name="acc")
            for g in range(NB):
                mm(acc, m, xq, xs, "wg", j, g, g == 0, g == NB - 1)
            nc.scalar.activation(out=s_sb[(m, j)][:], in_=acc[:], func=ACT.Sigmoid)

        st = {}

        def h_steps(j):
            def f1(m):
                acc = acc_pool.tile([P, BLK], F32, name="acc")
                for g in range(NB):
                    mm(acc, m, xq, xs, "wc1", j, g, g == 0, g == NB - 1)
                st[("f1", m)] = acc

            def a(m):
                h = elem.tile([P, BLK], F32, name="h")
                nc.vector.tensor_tensor(out=h[:], in0=st[("f1", m)][:], in1=s_sb[(m, j)][:], op=ALU.mult)
                st[("h", m)] = h

            def t(m):
                ht = tr_pool.tile([P, 4, P], F32, name="bank")
                for k in range(4):
                    nc.tensor.transpose(ht[:, k, :], st[("h", m)][:, k::4], ident[:])
                st[("ht", m)] = ht

            def b(m):
                u = elem.tile([P, BLK], BF16, name="u", align_bytes=64)
                nc.vector.scalar_tensor_tensor(
                    out=u[:].rearrange("p (n t) -> p n t", t=4),
                    in0=st[("ht", m)][:].rearrange("p t n -> p n t"),
                    scalar=1.0,
                    in1=xgm[j][:, :, m * P : (m + 1) * P].rearrange("p t n -> p n t"),
                    op0=ALU.add, op1=ALU.mult,
                )
                st[("u", m)] = u

            def q(m):
                cols = slice(m * P, (m + 1) * P)
                nc.vector.quantize_mx(out=uq[j][:, cols].bitcast(FP8X4), scales=us[j][:, cols], in_=st[("u", m)][:])

            return [f1, a, t, b, q], [0, 1, 1, 2, 3]

        def f_steps(j):
            def f(m):
                acc = acc_pool.tile([P, BLK], F32, name="acc")
                for g in range(NB):
                    mm(acc, m, xq, xs, "wc1", j, g, g == 0, False)
                for g in range(NB):
                    mm(acc, m, uq, us, "wc2", j, g, False, g == NB - 1)
                st[("f", m)] = acc

            def c(m):
                h2 = elem.tile([P, BLK], F32, name="h2")
                nc.vector.tensor_tensor(out=h2[:], in0=st[("f", m)][:], in1=s_sb[(m, j)][:], op=ALU.mult)
                st[("h2", m)] = h2

            def d(m):
                o = elem.tile([P, BLK], F32, name="o")
                cols = slice(j * BLK, (j + 1) * BLK)
                nc.vector.scalar_tensor_tensor(
                    out=o[:], in0=st[("h2", m)][:], scalar=1.0, in1=x_sb[m][:, cols], op0=ALU.add, op1=ALU.mult
                )
                nc.sync.dma_start(out=out[m * P : (m + 1) * P, cols], in_=o[:])

            return [f, c, d], [0, 1, 2]

        def substeps(fns, lags):
            res = []
            for k in range(MT + max(lags)):
                res.append([(fn, k - lag) for fn, lag in zip(fns, lags) if 0 <= k - lag < MT])
            return res

        def run(step):
            for fn, m in step:
                fn(m)

        queue = []
        pend = {}
        for j in range(NB):
            pend[6 * j + GS] = [[(lambda m, j=j: gate(m, j), m)] for m in range(MT)]
            fns, lags = h_steps(j)
            pend.setdefault(6 * j + HS, []).extend(substeps(fns, lags))
            fns, lags = f_steps(j)
            pend.setdefault(FS + 3 * j, []).extend(substeps(fns, lags))

        widen(0)
        for i in range(len(units) + 1):
            load(i + LEAD)
            if i < len(units):
                interleave(i)
            if i + 1 < len(units):
                widen(i + 1)
            if queue:
                run(queue.pop(0))
            if i >= 1:
                quantise(i - 1)
            if i < 6:
                for t in range(2):
                    make_xgm(i // 2, 2 * (i % 2) + t)
            queue.extend(pend.get(i, []))
            if queue:
                run(queue.pop(0))
        for step in queue:
            run(step)
